import numpy as np
import ml_dtypes


def mxq(x, axis, fmt="e4m3"):
    dtype, down = {"e4m3": (ml_dtypes.float8_e4m3fn, 7), "e5m2": (ml_dtypes.float8_e5m2, 14)}[fmt]
    v = np.moveaxis(np.asarray(x, np.float32).astype(ml_dtypes.bfloat16).astype(np.float64), axis, -1)
    blocks = v.reshape(v.shape[:-1] + (-1, 32))
    amax = np.abs(blocks).max(-1, keepdims=True)
    byte = np.maximum(np.where(amax > 0, np.frexp(amax)[1] - 1 + 127, 0) - down, 1)
    scale = np.exp2(byte - 127.0)
    codes = (blocks / scale).astype(np.float32).astype(dtype).astype(np.float64)
    return np.moveaxis((codes * scale).reshape(v.shape), -1, axis)


WIDE = False


def mx_kscale(k):
    if not WIDE:
        return np.ones(k)
    levels = np.array([10, -10, 5, -5, 0])
    if k % 512:
        return np.exp2(np.random.permutation(np.resize(levels, k // 32))).repeat(32)
    a = np.empty((k // 512, 16))
    for p in range(k // 512):
        a[p, :8] = np.random.permutation(np.resize(levels, 8))
        for g in range(8):
            far = levels[np.abs(levels - a[p, g]) >= 10]
            a[p, g + 8] = far[np.random.randint(len(far))]
    return np.exp2(a.ravel()).repeat(32)


def f64(x):
    return np.asarray(x).astype(np.float64)


def striped(idx):
    return np.tile(idx.reshape(-1, 16).T, (8, 1)).astype(np.uint16)


def unstriped(offs):
    return offs[:16].T.reshape(-1).astype(np.int64)


E2M1 = np.array([0.0, 0.5, 1.0, 1.5, 2.0, 3.0, 4.0, 6.0, -0.0, -0.5, -1.0, -1.5, -2.0, -3.0, -4.0, -6.0])


def pack_weight(w, fmt):
    k, n = w.shape
    w = f64(np.asarray(w, np.float32).astype(ml_dtypes.bfloat16)).reshape(k // 32, 32, n)
    amax = np.abs(w).max(1)
    if fmt == "e4m3":
        byte = np.frexp(amax)[1] - 1 + 127 - 7
    else:
        mant, ex = np.frexp(amax / 6.0)
        byte = np.where(mant > 0.5, ex, ex - 1) + 127
    byte = np.clip(np.where(amax > 0, byte, 1), 1, 254)
    scaled = (w * np.exp2(127.0 - byte)[:, None, :]).reshape(k, n).astype(np.float32)
    by_word = np.ascontiguousarray(scaled.reshape(k // 512, 128, 4, n).transpose(0, 1, 3, 2))
    if fmt == "e4m3":
        words = by_word.astype(ml_dtypes.float8_e4m3fn).view(np.uint8)
    else:
        c = by_word.astype(ml_dtypes.float4_e2m1fn).view(np.uint8) & 0xF
        words = (c[..., 0::2] | (c[..., 1::2] << 4)).reshape(k // 512, 128, 2 * n)
    return np.ascontiguousarray(words), np.ascontiguousarray(byte.astype(np.uint8).reshape(k // 512, 16, n))


def unpack_weight(words, scales, fmt):
    g, _, n = scales.shape
    words = np.ascontiguousarray(words).reshape(g, 128, n, -1)
    if fmt == "e4m3":
        vals = words.view(ml_dtypes.float8_e4m3fn).astype(np.float64)
    else:
        nib = np.empty((g, 128, n, 4), np.uint8)
        nib[..., 0::2] = words & 0xF
        nib[..., 1::2] = words >> 4
        vals = E2M1[nib]
    vals = vals * np.repeat(np.exp2(scales.astype(np.float64) - 127.0), 8, axis=1)[..., None]
    return vals.transpose(0, 1, 3, 2).reshape(g * 512, n)


def gelu(v):
    return 0.5 * v * (1.0 + np.tanh(np.sqrt(2.0 / np.pi) * (v + 0.044715 * v**3)))


def striped8(idx):
    return np.concatenate([v.reshape(-1, 16).T for v in idx]).astype(np.uint16)


def unstriped8(offs):
    return np.stack([offs[16 * g:16 * g + 16].T.reshape(-1) for g in range(8)]).astype(np.int64)


def runs(v, idx8):
    k = np.arange(v.shape[0])
    return v[k[:, None], idx8[k % 512 // 64]]


def often(T, S):
    return np.random.permutation(T)[(T * np.random.uniform(0, 1, S) ** 4).astype(np.int64)]


K, T, S, H = 1024, 2048, 1024, 512

def setup_inputs():
    n = np.random.standard_normal
    s = mx_kscale(K)[:, None]
    u = mx_kscale(H)[:, None]
    tab_words, tab_scales = pack_weight(n((K, T)) * s, "e4m3")
    offs = striped8(np.stack([often(T, S) for _ in range(8)]))
    w1 = 1.5 * H ** -0.25 * n((K, H)) / np.sqrt(K) / s * u.T
    w2_words, w2_scales = pack_weight(n((K, H)) / np.sqrt(K) / s, "e2m1")
    bias = 0.7 * H ** -0.25 * n(H) * u[:, 0]
    gain = H ** -0.25 * np.random.uniform(0.7, 1.8, H) / u[:, 0]
    mask = np.where(np.random.uniform(size=(S, S)) < 0.5, 0.0, -2.0)
    return {"tab_words": tab_words, "tab_scales": tab_scales, "offs": offs,
            "w1": w1.astype(np.float32),
            "w2_words": w2_words, "w2_scales": w2_scales,
            "bias": bias.astype(np.float32), "gain": gain.astype(np.float32),
            "mask": mask.astype(np.float32)}

def reference(tab_words, tab_scales, offs, w1, w2_words, w2_scales, bias, gain, mask):
    v = runs(unpack_weight(tab_words, tab_scales, "e4m3"), unstriped8(offs))
    goal = (mxq(f64(w1), 0, "e4m3").T @ v) + f64(bias)[:, None]
    w2 = unpack_weight(w2_words, w2_scales, "e2m1")
    hyp = f64(gain)[:, None] * np.tanh(w2.T @ v)
    goal_q = mxq(goal, 0, "e4m3")
    hyp_q = mxq(hyp, 0, "e4m3")
    e = (goal_q.T @ hyp_q) + f64(mask)
    return 1.0 / (1.0 + np.exp(-e))

@@ -1,0 +1,276 @@
+from contextlib import ExitStack
+
+import concourse.mybir as mybir
+from concourse.masks import make_identity
+
+K, T, S, H = 1024, 2048, 1024, 512
+FLOPS = 2 * K * H * S * 2 + 2 * H * S * S
+
+F32 = mybir.dt.float32
+BF16 = mybir.dt.bfloat16
+I32 = mybir.dt.int32
+U32 = mybir.dt.uint32
+U16 = mybir.dt.uint16
+U8 = mybir.dt.uint8
+E4M3 = mybir.dt.float8_e4m3fn_x4
+E2M1 = mybir.dt.float4_e2m1fn_x4
+ACT = mybir.ActivationFunctionType
+ALU = mybir.AluOpType
+
+P = 128
+PASSES = 2
+SLOTS = 4
+CHUNK = 128
+BANK = 512
+
+
+def tile_list_proof_state_pairing_kernel(
+    tc, tab_words, tab_scales, offs, w1, w2_words, w2_scales, bias, gain, mask, out
+):
+    nc = tc.nc
+    with ExitStack() as ctx:
+        keep = ctx.enter_context(tc.tile_pool(name="keep", bufs=1))
+        ring = ctx.enter_context(tc.tile_pool(name="ring", bufs=3))
+        psum = ctx.enter_context(tc.psum_pool(name="psum", bufs=8))
+
+        scale_table = keep.tile([P, T], U8, name="scale_table", tag="scale_table", align_bytes=64)
+        nc.gpsimd.memset(scale_table[:].bitcast(I32), 0)
+
+        lists = keep.tile([P, S // 16], U16, name="lists")
+        nc.sync.dma_start(lists[:], offs)
+        w2_raw = keep.tile([P, PASSES, 256], I32, name="w2_raw", tag="w2_raw")
+        nc.sync.dma_start(w2_raw[:], w2_words.rearrange("a p c -> p a c").bitcast(I32))
+        coef_rows = keep.tile([P, P], F32, name="coef_rows")
+        first = P - 2 * SLOTS
+        for i, vec in enumerate((bias, gain)):
+            nc.sync.dma_start(
+                coef_rows[first + SLOTS * i : first + SLOTS * (i + 1), :].rearrange("t (b i) -> t b i", i=8),
+                vec.rearrange("(b t i) -> t b i", t=SLOTS, i=8),
+            )
+        for a in range(PASSES):
+            nc.sync.dma_start(scale_table[a:P:8, :].bitcast(I32), tab_scales[a].bitcast(I32))
+        table = []
+        for a in range(PASSES):
+            words = keep.tile([P, T], U32, name="table%d" % a, tag="table%d" % a, align_bytes=64)
+            nc.sync.dma_start(
+                words[:].bitcast(I32), tab_words[a].rearrange("p t i -> p (t i)").bitcast(I32)
+            )
+            table.append(words)
+
+        warm = keep.tile([P, 2], F32, name="warm")
+        nc.vector.memset(warm[:, 0:1], 0.0)
+        nc.scalar.activation(warm[:, 1:2], warm[:, 0:1], ACT.Sigmoid)
+
+        w2s_raw = keep.tile([P, PASSES * H], U8, name="w2s_raw", tag="w2s_raw", align_bytes=64)
+        nc.vector.memset(w2s_raw[:].bitcast(I32), 0)
+        nc.vector.memset(coef_rows[0:first, :], 0.0)
+        v_scales = keep.tile([P, PASSES * S], U8, name="v_scales", align_bytes=64)
+        nc.vector.memset(v_scales[:].bitcast(I32), 0)
+
+        ident = keep.tile([P, P], F32, name="ident")
+        make_identity(nc, ident[:])
+
+        w2s_rows = w2_scales.rearrange("a (d r) c -> r d a c", r=4)
+        for r in range(4):
+            nc.gpsimd.dma_start(
+                w2s_raw[r:P:32, :].bitcast(I32).rearrange("d (a w) -> d a w", a=PASSES),
+                w2s_rows[r].bitcast(I32),
+            )
+
+        picked_scales = keep.tile([P, S], U8, name="picked_scales", align_bytes=64)
+        nc.vector.tensor_copy(picked_scales[:], scale_table[:].indirect(lists[:]))
+        for a in range(PASSES):
+            for r in range(4):
+                nc.scalar.dma_start(
+                    v_scales[r:P:32, a * S : (a + 1) * S].bitcast(I32),
+                    picked_scales[8 * r + a : P : 32, :].bitcast(I32),
+                )
+        w2_codes = keep.tile([P, PASSES * 2 * H], U8, name="w2_codes", tag="scale_table", align_bytes=64)
+        nc.vector.tensor_copy(
+            w2_codes[:].bitcast(I32).rearrange("p (a t b i) -> p a t b i", a=PASSES, t=SLOTS, i=4),
+            w2_raw[:].rearrange("p a (b t i) -> p a t b i", t=SLOTS, i=4),
+        )
+        w1_raw = []
+        raw0 = keep.tile([P, SLOTS * H], F32, name="w1_raw0", tag="w2_raw")
+        nc.sync.dma_start(raw0[:], w1[0:512, :].rearrange("(p j) c -> p (j c)", j=4))
+        w1_raw.append(raw0)
+
+        coef_bank = psum.tile([P, BANK], F32, name="coef_bank", tag="bank")
+        nc.tensor.transpose(coef_bank[:, 0:P], coef_rows[:], ident[:])
+        coef = keep.tile([P, 2 * SLOTS], F32, name="coef")
+        nc.scalar.copy(coef[:], coef_bank[:, first:P])
+
+        v_words = [keep.tile([P, S], U32, name="v_words0", align_bytes=64)]
+        nc.vector.tensor_copy(v_words[0][:], table[0][:].indirect(lists[:]))
+
+        w2_planes = keep.tile([P, PASSES * H], U8, name="w2_planes", align_bytes=64)
+        nc.vector.tensor_copy(
+            w2_planes[:].bitcast(I32).rearrange("p (a t b i) -> p a t b i", a=PASSES, t=SLOTS, i=2),
+            w2s_raw[:].bitcast(I32).rearrange("p (a b t i) -> p a t b i", a=PASSES, t=SLOTS, i=2),
+        )
+
+        raw1 = keep.tile([P, SLOTS * H], F32, name="w1_raw1", tag="table0", align_bytes=64)
+        nc.sync.dma_start(raw1[:], w1[512:1024, :].rearrange("(p j) c -> p (j c)", j=4))
+        w1_raw.append(raw1)
+
+        v_words.append(keep.tile([P, S], U32, name="v_words1", tag="w2s_raw", align_bytes=64))
+        for c0, c1 in ((0, 256), (256, 512), (512, 1024)):
+            nc.vector.tensor_copy(
+                v_words[1][:, c0:c1], table[1][:].indirect(lists[:, c0 // 16 : c1 // 16])
+            )
+
+        masks_sb = keep.tile([P, S // P, S], F32, name="masks_sb", tag="table1", align_bytes=64)
+        for m in range(S // P):
+            nc.sync.dma_start(masks_sb[:, m, :], mask[m * P : (m + 1) * P, :])
+
+        w1_bf = [keep.tile([P, SLOTS * H], BF16, name="w1_bf0", align_bytes=64)]
+        w1_codes = [keep.tile([P, H], U32, name="w1_codes%d" % a, align_bytes=64) for a in range(PASSES)]
+        w1_planes = [keep.tile([P, H], U8, name="w1_planes%d" % a, align_bytes=64) for a in range(PASSES)]
+
+        def round_w1(a, t, copy):
+            src = w1_raw[a][:].rearrange("p (j b t h l) -> p t b h j l", j=4, t=SLOTS, h=2, l=4)
+            dst = w1_bf[a][:].rearrange("p (t b h l j) -> p t b h j l", j=4, t=SLOTS, h=2, l=4)
+            copy(dst[:, t], src[:, t])
+
+        def quantise(codes, planes, values, c0, c1):
+            nc.vector.quantize_mx(
+                out=codes[:, c0:c1].bitcast(E4M3), scales=planes[:, c0:c1], in_=values[:, 4 * c0 : 4 * c1]
+            )
+
+        def stage_one(bank_view, t, c0, c1, on_w1):
+            for a in range(PASSES):
+                if on_w1:
+                    lhsT = w1_codes[a][:, t * P : (t + 1) * P].bitcast(E4M3)
+                    lhsT_scale = w1_planes[a][:, t * P : (t + 1) * P]
+                else:
+                    lhsT = w2_codes[:, a * 2 * H + t * 2 * P : a * 2 * H + (t + 1) * 2 * P].bitcast(E2M1)
+                    lhsT_scale = w2_planes[:, a * H + t * P : a * H + (t + 1) * P]
+                nc.tensor.matmul_mx(
+                    out=bank_view,
+                    lhsT=lhsT,
+                    lhsT_scale=lhsT_scale,
+                    rhs=v_words[a][:, c0:c1].bitcast(E4M3),
+                    rhs_scale=v_scales[:, a * S + c0 : a * S + c1],
+                    start=(a == 0),
+                    stop=(a == PASSES - 1),
+                )
+
+        hyp_tanh = [
+            keep.tile([P, SLOTS * 256], F32, name="hyp_tanh%d" % q, tag="hyp_tanh%d" % q, align_bytes=64)
+            for q in range(4)
+        ]
+        hyp_bf = keep.tile([P, SLOTS * S], BF16, name="hyp_bf", align_bytes=64)
+        hyp_codes = keep.tile([P, S], U32, name="hyp_codes", align_bytes=64)
+        hyp_planes = keep.tile([P, S], U8, name="hyp_planes", align_bytes=64)
+        goal_bf = keep.tile([P, SLOTS * S], BF16, name="goal_bf", align_bytes=64)
+        goal_codes = keep.tile([P, S], U32, name="goal_codes", align_bytes=64)
+        goal_planes = keep.tile([P, S], U8, name="goal_planes", align_bytes=64)
+
+        def hyp_chunk(c):
+            c0, c1 = c * CHUNK, (c + 1) * CHUNK
+            bank = psum.tile([P, BANK], F32, name="hyp_bank", tag="bank")
+            for t in range(SLOTS):
+                stage_one(bank[:, t * CHUNK : (t + 1) * CHUNK], t, c0, c1, False)
+            nc.scalar.activation(
+                hyp_tanh[c // 2][:, (c % 2) * BANK : (c % 2 + 1) * BANK].rearrange("p (n t) -> p n t", t=SLOTS),
+                bank[:].rearrange("p (t n) -> p n t", t=SLOTS),
+                ACT.Tanh,
+            )
+
+        def hyp_gain(c0, c1):
+            nc.vector.tensor_tensor(
+                hyp_bf[:, 4 * c0 : 4 * c1].rearrange("p (n t) -> p n t", t=SLOTS),
+                hyp_tanh[c0 // 256][:].rearrange("p (n t) -> p n t", t=SLOTS),
+                coef[:, SLOTS : 2 * SLOTS].unsqueeze(1).to_broadcast([P, c1 - c0, SLOTS]),
+                ALU.mult,
+            )
+
+        def goal_chunk(c):
+            c0, c1 = c * CHUNK, (c + 1) * CHUNK
+            bank = psum.tile([P, BANK], F32, name="goal_bank", tag="bank")
+            for t in range(SLOTS):
+                stage_one(bank[:, t * CHUNK : (t + 1) * CHUNK], t, c0, c1, True)
+            nc.vector.tensor_tensor(
+                goal_bf[:, 4 * c0 : 4 * c1].rearrange("p (n t) -> p n t", t=SLOTS),
+                bank[:].rearrange("p (t n) -> p n t", t=SLOTS),
+                coef[:, 0:SLOTS].unsqueeze(1).to_broadcast([P, CHUNK, SLOTS]),
+                ALU.add,
+            )
+
+        goal_rows = keep.tile([P, SLOTS * S], BF16, name="goal_rows")
+
+        def goal_wide(c0, c1):
+            width = c1 - c0
+            per_bank = BANK // width
+            for t0 in range(0, SLOTS, per_bank):
+                bank = psum.tile([P, BANK], F32, name="goal_bank", tag="bank")
+                for t in range(t0, t0 + per_bank):
+                    stage_one(bank[:, (t - t0) * width : (t - t0 + 1) * width], t, c0, c1, True)
+                for t in range(t0, t0 + per_bank):
+                    nc.scalar.activation(
+                        goal_rows[:, 4 * c0 + t * width : 4 * c0 + (t + 1) * width],
+                        bank[:, (t - t0) * width : (t - t0 + 1) * width],
+                        ACT.Identity,
+                        bias=coef[:, t : t + 1],
+                    )
+
+        def goal_weave(c0, c1):
+            nc.vector.tensor_copy(
+                goal_bf[:, 4 * c0 : 4 * c1].rearrange("p (n l t) -> p n t l", t=SLOTS, l=4),
+                goal_rows[:, 4 * c0 : 4 * c1].rearrange("p (t n l) -> p n t l", t=SLOTS, l=4),
+            )
+
+        def score(m):
+            result = ring.tile([P, S], F32, name="result")
+            for h in range(S // BANK):
+                cols = slice(h * BANK, (h + 1) * BANK)
+                bank = psum.tile([P, BANK], F32, name="score_bank", tag="bank")
+                nc.tensor.matmul_mx(
+                    out=bank[:],
+                    lhsT=goal_codes[:, m * P : (m + 1) * P].bitcast(E4M3),
+                    lhsT_scale=goal_planes[:, m * P : (m + 1) * P],
+                    rhs=hyp_codes[:, cols].bitcast(E4M3),
+                    rhs_scale=hyp_planes[:, cols],
+                    start=True,
+                    stop=True,
+                )
+                logits = ring.tile([P, BANK], F32, name="logits", bufs=4)
+                nc.vector.tensor_tensor(logits[:], bank[:], masks_sb[:, m, cols], ALU.add)
+                nc.scalar.activation(result[:, cols], logits[:], ACT.Sigmoid)
+                if m == S // P - 1:
+                    nc.sync.dma_start(out[m * P : (m + 1) * P, cols], result[:, cols])
+            if m < S // P - 1:
+                nc.sync.dma_start(out[m * P : (m + 1) * P, :], result[:])
+
+        for c in range(4):
+            hyp_chunk(c)
+        for t in range(SLOTS):
+            round_w1(0, t, nc.vector.tensor_copy)
+        hyp_gain(0, 256)
+        quantise(w1_codes[0], w1_planes[0], w1_bf[0], 0, H)
+        hyp_gain(256, 512)
+        w1_bf.append(keep.tile([P, SLOTS * H], BF16, name="w1_bf1", tag="hyp_tanh0", align_bytes=64))
+        for t in range(SLOTS):
+            round_w1(1, t, nc.scalar.copy)
+        quantise(hyp_codes, hyp_planes, hyp_bf, 0, 512)
+        quantise(w1_codes[1], w1_planes[1], w1_bf[1], 0, 256)
+        quantise(w1_codes[1], w1_planes[1], w1_bf[1], 256, 512)
+        for c in range(4, 8):
+            hyp_chunk(c)
+        goal_chunk(0)
+        goal_chunk(1)
+        goal_wide(256, 512)
+        hyp_gain(512, 768)
+        quantise(goal_codes, goal_planes, goal_bf, 0, 256)
+        hyp_gain(768, 1024)
+        goal_wide(512, 1024)
+        goal_weave(256, 512)
+        quantise(hyp_codes, hyp_planes, hyp_bf, 512, 1024)
+        quantise(goal_codes, goal_planes, goal_bf, 256, 512)
+        score(0)
+        score(1)
+        goal_weave(512, 1024)
+        score(2)
+        quantise(goal_codes, goal_planes, goal_bf, 512, 1024)
+        for m in range(3, 8):
+            score(m)

@@ -36,62 +36,68 @@ def tile_list_proof_state_pairing_kernel(
         scale_table = keep.tile([P, T], U8, name="scale_table", tag="scale_table", align_bytes=64)
         nc.gpsimd.memset(scale_table[:].bitcast(I32), 0)
 
+        w2_raw = keep.tile([P, PASSES, 256], I32, name="w2_raw", tag="w2_raw", align_bytes=64)
+        nc.sync.dma_start(w2_raw[:], w2_words.rearrange("a p c -> p a c").bitcast(I32))
         lists = keep.tile([P, S // 16], U16, name="lists")
         nc.sync.dma_start(lists[:], offs)
-        w2_raw = keep.tile([P, PASSES, 256], I32, name="w2_raw", tag="w2_raw")
-        nc.sync.dma_start(w2_raw[:], w2_words.rearrange("a p c -> p a c").bitcast(I32))
-        coef_rows = keep.tile([P, P], F32, name="coef_rows")
-        first = P - 2 * SLOTS
-        for i, vec in enumerate((bias, gain)):
+        w2s_raw = keep.tile([P, PASSES * H], U8, name="w2s_raw", tag="w2s_raw", align_bytes=64)
+        nc.vector.memset(w2s_raw[:].bitcast(I32), 0)
+        w2s_rows = w2_scales.rearrange("a (d r) c -> d r a c", r=4)
+
+        def load_w2_scales(d):
             nc.sync.dma_start(
-                coef_rows[first + SLOTS * i : first + SLOTS * (i + 1), :].rearrange("t (b i) -> t b i", i=8),
-                vec.rearrange("(b t i) -> t b i", t=SLOTS, i=8),
+                w2s_raw[32 * d : 32 * d + 4, :].bitcast(I32).rearrange("r (a w) -> r a w", a=PASSES),
+                w2s_rows[d].bitcast(I32),
             )
+
+        tab_rows = tab_scales.rearrange("a (g e) t -> a e g t", e=2)
         for a in range(PASSES):
-            nc.sync.dma_start(scale_table[a:P:8, :].bitcast(I32), tab_scales[a].bitcast(I32))
+            for e in range(2):
+                nc.sync.dma_start(
+                    scale_table[2 * a + e : P : 16, :].bitcast(I32), tab_rows[a, e].bitcast(I32)
+                )
         table = []
         for a in range(PASSES):
+            for d in ((0,), (1, 2, 3))[a]:
+                load_w2_scales(d)
             words = keep.tile([P, T], U32, name="table%d" % a, tag="table%d" % a, align_bytes=64)
             nc.sync.dma_start(
                 words[:].bitcast(I32), tab_words[a].rearrange("p t i -> p (t i)").bitcast(I32)
             )
             table.append(words)
 
+        coef_rows = keep.tile([P, P], F32, name="coef_rows")
+        first = P - 2 * SLOTS
+        for i, vec in enumerate((bias, gain)):
+            nc.gpsimd.dma_start(
+                coef_rows[first + SLOTS * i : first + SLOTS * (i + 1), :].rearrange("t (u l) -> t u l", l=4),
+                vec.rearrange("(u t l) -> t u l", t=SLOTS, l=4),
+            )
+
         warm = keep.tile([P, 2], F32, name="warm")
         nc.vector.memset(warm[:, 0:1], 0.0)
         nc.scalar.activation(warm[:, 1:2], warm[:, 0:1], ACT.Sigmoid)
 
-        w2s_raw = keep.tile([P, PASSES * H], U8, name="w2s_raw", tag="w2s_raw", align_bytes=64)
-        nc.vector.memset(w2s_raw[:].bitcast(I32), 0)
         nc.vector.memset(coef_rows[0:first, :], 0.0)
         v_scales = keep.tile([P, PASSES * S], U8, name="v_scales", align_bytes=64)
-        nc.vector.memset(v_scales[:].bitcast(I32), 0)
+        nc.vector.memset(v_scales[:, S : 2 * S].bitcast(I32), 0)
+        w2_planes = keep.tile([P, PASSES * H], U8, name="w2_planes", align_bytes=64)
 
         ident = keep.tile([P, P], F32, name="ident")
         make_identity(nc, ident[:])
 
-        w2s_rows = w2_scales.rearrange("a (d r) c -> r d a c", r=4)
-        for r in range(4):
-            nc.gpsimd.dma_start(
-                w2s_raw[r:P:32, :].bitcast(I32).rearrange("d (a w) -> d a w", a=PASSES),
-                w2s_rows[r].bitcast(I32),
-            )
-
         picked_scales = keep.tile([P, S], U8, name="picked_scales", align_bytes=64)
         nc.vector.tensor_copy(picked_scales[:], scale_table[:].indirect(lists[:]))
+        nc.vector.tensor_copy(v_scales[:, 0:S].bitcast(I32), picked_scales[:].bitcast(I32))
         for a in range(PASSES):
             for r in range(4):
-                nc.scalar.dma_start(
-                    v_scales[r:P:32, a * S : (a + 1) * S].bitcast(I32),
-                    picked_scales[8 * r + a : P : 32, :].bitcast(I32),
-                )
-        w2_codes = keep.tile([P, PASSES * 2 * H], U8, name="w2_codes", tag="scale_table", align_bytes=64)
-        nc.vector.tensor_copy(
-            w2_codes[:].bitcast(I32).rearrange("p (a t b i) -> p a t b i", a=PASSES, t=SLOTS, i=4),
-            w2_raw[:].rearrange("p a (b t i) -> p a t b i", t=SLOTS, i=4),
-        )
+                if a > 0 or r >= 2:
+                    nc.sync.dma_start(
+                        v_scales[r:P:32, a * S : (a + 1) * S].bitcast(I32),
+                        picked_scales[16 * (r // 2) + 2 * a + r % 2 : P : 32, :].bitcast(I32),
+                    )
         w1_raw = []
-        raw0 = keep.tile([P, SLOTS * H], F32, name="w1_raw0", tag="w2_raw")
+        raw0 = keep.tile([P, SLOTS * H], F32, name="w1_raw0", tag="scale_table", align_bytes=64)
         nc.sync.dma_start(raw0[:], w1[0:512, :].rearrange("(p j) c -> p (j c)", j=4))
         w1_raw.append(raw0)
 
@@ -103,17 +109,20 @@ def tile_list_proof_state_pairing_kernel(
         v_words = [keep.tile([P, S], U32, name="v_words0", align_bytes=64)]
         nc.vector.tensor_copy(v_words[0][:], table[0][:].indirect(lists[:]))
 
-        w2_planes = keep.tile([P, PASSES * H], U8, name="w2_planes", align_bytes=64)
         nc.vector.tensor_copy(
-            w2_planes[:].bitcast(I32).rearrange("p (a t b i) -> p a t b i", a=PASSES, t=SLOTS, i=2),
-            w2s_raw[:].bitcast(I32).rearrange("p (a b t i) -> p a t b i", a=PASSES, t=SLOTS, i=2),
+            w2_planes[:].bitcast(I32).rearrange("p (a t u) -> p a t u", a=PASSES, t=SLOTS),
+            w2s_raw[:].bitcast(I32).rearrange("p (a u t) -> p a t u", a=PASSES, t=SLOTS),
         )
-
-        raw1 = keep.tile([P, SLOTS * H], F32, name="w1_raw1", tag="table0", align_bytes=64)
+        w2_codes = keep.tile([P, PASSES * 2 * H], U8, name="w2_codes", tag="table0", align_bytes=64)
+        nc.vector.tensor_copy(
+            w2_codes[:].bitcast(I32).rearrange("p (a t u w) -> p a t u w", a=PASSES, t=SLOTS, w=2),
+            w2_raw[:].rearrange("p a (u t w) -> p a t u w", t=SLOTS, w=2),
+        )
+        raw1 = keep.tile([P, SLOTS * H], F32, name="w1_raw1", tag="w2_raw", align_bytes=64)
         nc.sync.dma_start(raw1[:], w1[512:1024, :].rearrange("(p j) c -> p (j c)", j=4))
         w1_raw.append(raw1)
 
-        v_words.append(keep.tile([P, S], U32, name="v_words1", tag="w2s_raw", align_bytes=64))
+        v_words.append(keep.tile([P, S], U32, name="v_words1", align_bytes=64))
         for c0, c1 in ((0, 256), (256, 512), (512, 1024)):
             nc.vector.tensor_copy(
                 v_words[1][:, c0:c1], table[1][:].indirect(lists[:, c0 // 16 : c1 // 16])
@@ -123,89 +132,102 @@ def tile_list_proof_state_pairing_kernel(
         for m in range(S // P):
             nc.sync.dma_start(masks_sb[:, m, :], mask[m * P : (m + 1) * P, :])
 
-        w1_bf = [keep.tile([P, SLOTS * H], BF16, name="w1_bf0", align_bytes=64)]
+        w1_bf = [keep.tile([P, SLOTS * H], BF16, name="w1_bf%d" % a, align_bytes=64) for a in range(PASSES)]
         w1_codes = [keep.tile([P, H], U32, name="w1_codes%d" % a, align_bytes=64) for a in range(PASSES)]
         w1_planes = [keep.tile([P, H], U8, name="w1_planes%d" % a, align_bytes=64) for a in range(PASSES)]
 
-        def round_w1(a, t, copy):
-            src = w1_raw[a][:].rearrange("p (j b t h l) -> p t b h j l", j=4, t=SLOTS, h=2, l=4)
-            dst = w1_bf[a][:].rearrange("p (t b h l j) -> p t b h j l", j=4, t=SLOTS, h=2, l=4)
-            copy(dst[:, t], src[:, t])
+        def round_w1(a):
+            nc.vector.tensor_copy(
+                w1_bf[a][:].rearrange("p (t u l j) -> p t u j l", t=SLOTS, l=4, j=4),
+                w1_raw[a][:].rearrange("p (j u t l) -> p t u j l", t=SLOTS, l=4, j=4),
+            )
 
         def quantise(codes, planes, values, c0, c1):
             nc.vector.quantize_mx(
                 out=codes[:, c0:c1].bitcast(E4M3), scales=planes[:, c0:c1], in_=values[:, 4 * c0 : 4 * c1]
             )
 
-        def stage_one(bank_view, t, c0, c1, on_w1):
+        def w1_operand(a, t):
+            cols = slice(t * P, (t + 1) * P)
+            return w1_codes[a][:, cols].bitcast(E4M3), w1_planes[a][:, cols]
+
+        def w2_operand(a, t):
+            col = a * H + t * P
+            return w2_codes[:, 2 * col : 2 * (col + P)].bitcast(E2M1), w2_planes[:, col : col + P]
+
+        def project(bank_cols, operand, t, c0, c1):
             for a in range(PASSES):
-                if on_w1:
-                    lhsT = w1_codes[a][:, t * P : (t + 1) * P].bitcast(E4M3)
-                    lhsT_scale = w1_planes[a][:, t * P : (t + 1) * P]
-                else:
-                    lhsT = w2_codes[:, a * 2 * H + t * 2 * P : a * 2 * H + (t + 1) * 2 * P].bitcast(E2M1)
-                    lhsT_scale = w2_planes[:, a * H + t * P : a * H + (t + 1) * P]
+                codes, plane = operand(a, t)
                 nc.tensor.matmul_mx(
-                    out=bank_view,
-                    lhsT=lhsT,
-                    lhsT_scale=lhsT_scale,
+                    out=bank_cols,
+                    lhsT=codes,
+                    lhsT_scale=plane,
                     rhs=v_words[a][:, c0:c1].bitcast(E4M3),
                     rhs_scale=v_scales[:, a * S + c0 : a * S + c1],
                     start=(a == 0),
                     stop=(a == PASSES - 1),
                 )
 
-        hyp_tanh = [
-            keep.tile([P, SLOTS * 256], F32, name="hyp_tanh%d" % q, tag="hyp_tanh%d" % q, align_bytes=64)
-            for q in range(4)
-        ]
-        hyp_bf = keep.tile([P, SLOTS * S], BF16, name="hyp_bf", align_bytes=64)
+        def project_narrow(operand, c0):
+            bank = psum.tile([P, BANK], F32, name="bank", tag="bank")
+            for t in range(SLOTS):
+                project(bank[:, t * CHUNK : (t + 1) * CHUNK], operand, t, c0, c0 + CHUNK)
+            return bank[:].rearrange("p (t n) -> p n t", t=SLOTS)
+
+        def woven(tile, c0, c1):
+            return tile[:, 4 * c0 : 4 * c1].rearrange("p (n t) -> p n t", t=SLOTS)
+
+        def weave(dst, rows, c0, c1):
+            nc.vector.tensor_copy(
+                dst[:, 4 * c0 : 4 * c1].rearrange("p (n l t) -> p n t l", t=SLOTS, l=4),
+                rows[:, 4 * c0 : 4 * c1].rearrange("p (t n l) -> p n t l", t=SLOTS, l=4),
+            )
+
+        hyp_tanh = keep.tile([P, SLOTS * S], F32, name="hyp_tanh")
+        hyp_rows = keep.tile([P, SLOTS * S], BF16, name="hyp_rows")
         hyp_codes = keep.tile([P, S], U32, name="hyp_codes", align_bytes=64)
         hyp_planes = keep.tile([P, S], U8, name="hyp_planes", align_bytes=64)
+        goal_rows = keep.tile([P, SLOTS * S], BF16, name="goal_rows")
         goal_bf = keep.tile([P, SLOTS * S], BF16, name="goal_bf", align_bytes=64)
         goal_codes = keep.tile([P, S], U32, name="goal_codes", align_bytes=64)
         goal_planes = keep.tile([P, S], U8, name="goal_planes", align_bytes=64)
 
-        def hyp_chunk(c):
-            c0, c1 = c * CHUNK, (c + 1) * CHUNK
-            bank = psum.tile([P, BANK], F32, name="hyp_bank", tag="bank")
-            for t in range(SLOTS):
-                stage_one(bank[:, t * CHUNK : (t + 1) * CHUNK], t, c0, c1, False)
-            nc.scalar.activation(
-                hyp_tanh[c // 2][:, (c % 2) * BANK : (c % 2 + 1) * BANK].rearrange("p (n t) -> p n t", t=SLOTS),
-                bank[:].rearrange("p (t n) -> p n t", t=SLOTS),
-                ACT.Tanh,
-            )
+        def hyp_narrow(c0):
+            nc.scalar.activation(woven(hyp_tanh, c0, c0 + CHUNK), project_narrow(w2_operand, c0), ACT.Tanh)
 
         def hyp_gain(c0, c1):
             nc.vector.tensor_tensor(
-                hyp_bf[:, 4 * c0 : 4 * c1].rearrange("p (n t) -> p n t", t=SLOTS),
-                hyp_tanh[c0 // 256][:].rearrange("p (n t) -> p n t", t=SLOTS),
+                woven(hyp_bf, c0, c1),
+                woven(hyp_tanh, c0, c1),
                 coef[:, SLOTS : 2 * SLOTS].unsqueeze(1).to_broadcast([P, c1 - c0, SLOTS]),
                 ALU.mult,
             )
 
-        def goal_chunk(c):
-            c0, c1 = c * CHUNK, (c + 1) * CHUNK
-            bank = psum.tile([P, BANK], F32, name="goal_bank", tag="bank")
+        def hyp_wide(c0):
             for t in range(SLOTS):
-                stage_one(bank[:, t * CHUNK : (t + 1) * CHUNK], t, c0, c1, True)
+                bank = psum.tile([P, BANK], F32, name="bank", tag="bank")
+                project(bank[:], w2_operand, t, c0, c0 + BANK)
+                row = slice(4 * c0 + t * BANK, 4 * c0 + (t + 1) * BANK)
+                nc.scalar.activation(hyp_tanh[:, row], bank[:], ACT.Tanh)
+                nc.scalar.activation(
+                    hyp_rows[:, row], hyp_tanh[:, row], ACT.Copy, scale=coef[:, SLOTS + t : SLOTS + t + 1]
+                )
+
+        def goal_narrow(c0):
             nc.vector.tensor_tensor(
-                goal_bf[:, 4 * c0 : 4 * c1].rearrange("p (n t) -> p n t", t=SLOTS),
-                bank[:].rearrange("p (t n) -> p n t", t=SLOTS),
+                woven(goal_bf, c0, c0 + CHUNK),
+                project_narrow(w1_operand, c0),
                 coef[:, 0:SLOTS].unsqueeze(1).to_broadcast([P, CHUNK, SLOTS]),
                 ALU.add,
             )
-
-        goal_rows = keep.tile([P, SLOTS * S], BF16, name="goal_rows")
 
         def goal_wide(c0, c1):
             width = c1 - c0
             per_bank = BANK // width
             for t0 in range(0, SLOTS, per_bank):
-                bank = psum.tile([P, BANK], F32, name="goal_bank", tag="bank")
+                bank = psum.tile([P, BANK], F32, name="bank", tag="bank")
                 for t in range(t0, t0 + per_bank):
-                    stage_one(bank[:, (t - t0) * width : (t - t0 + 1) * width], t, c0, c1, True)
+                    project(bank[:, (t - t0) * width : (t - t0 + 1) * width], w1_operand, t, c0, c1)
                 for t in range(t0, t0 + per_bank):
                     nc.scalar.activation(
                         goal_rows[:, 4 * c0 + t * width : 4 * c0 + (t + 1) * width],
@@ -214,63 +236,63 @@ def tile_list_proof_state_pairing_kernel(
                         bias=coef[:, t : t + 1],
                     )
 
-        def goal_weave(c0, c1):
-            nc.vector.tensor_copy(
-                goal_bf[:, 4 * c0 : 4 * c1].rearrange("p (n l t) -> p n t l", t=SLOTS, l=4),
-                goal_rows[:, 4 * c0 : 4 * c1].rearrange("p (t n l) -> p n t l", t=SLOTS, l=4),
+        results = {}
+
+        def score(m, h):
+            if m not in results:
+                results[m] = ring.tile([P, S], F32, name="result", bufs=4)
+            result = results[m]
+            rows, cols = slice(m * P, (m + 1) * P), slice(h * BANK, (h + 1) * BANK)
+            bank = psum.tile([P, BANK], F32, name="bank", tag="bank")
+            nc.tensor.matmul_mx(
+                out=bank[:],
+                lhsT=goal_codes[:, rows].bitcast(E4M3),
+                lhsT_scale=goal_planes[:, rows],
+                rhs=hyp_codes[:, cols].bitcast(E4M3),
+                rhs_scale=hyp_planes[:, cols],
+                start=True,
+                stop=True,
             )
+            last = m == S // P - 1 and h == 1
+            width = BANK // 2 if last else BANK
+            for u0 in range(0, BANK, width):
+                part = slice(h * BANK + u0, h * BANK + u0 + width)
+                logits = ring.tile([P, width], F32, name="logits", bufs=6)
+                nc.vector.tensor_tensor(logits[:], bank[:, u0 : u0 + width], masks_sb[:, m, part], ALU.add)
+                nc.scalar.activation(result[:, part], logits[:], ACT.Sigmoid)
+                if m >= S // P - 2:
+                    nc.sync.dma_start(out[rows, part], result[:, part])
+            if m < S // P - 2 and h == 1:
+                nc.sync.dma_start(out[rows, :], result[:])
 
-        def score(m):
-            result = ring.tile([P, S], F32, name="result")
-            for h in range(S // BANK):
-                cols = slice(h * BANK, (h + 1) * BANK)
-                bank = psum.tile([P, BANK], F32, name="score_bank", tag="bank")
-                nc.tensor.matmul_mx(
-                    out=bank[:],
-                    lhsT=goal_codes[:, m * P : (m + 1) * P].bitcast(E4M3),
-                    lhsT_scale=goal_planes[:, m * P : (m + 1) * P],
-                    rhs=hyp_codes[:, cols].bitcast(E4M3),
-                    rhs_scale=hyp_planes[:, cols],
-                    start=True,
-                    stop=True,
-                )
-                logits = ring.tile([P, BANK], F32, name="logits", bufs=4)
-                nc.vector.tensor_tensor(logits[:], bank[:], masks_sb[:, m, cols], ALU.add)
-                nc.scalar.activation(result[:, cols], logits[:], ACT.Sigmoid)
-                if m == S // P - 1:
-                    nc.sync.dma_start(out[m * P : (m + 1) * P, cols], result[:, cols])
-            if m < S // P - 1:
-                nc.sync.dma_start(out[m * P : (m + 1) * P, :], result[:])
-
-        for c in range(4):
-            hyp_chunk(c)
-        for t in range(SLOTS):
-            round_w1(0, t, nc.vector.tensor_copy)
-        hyp_gain(0, 256)
+        round_w1(0)
+        for c0 in range(0, BANK, CHUNK):
+            hyp_narrow(c0)
         quantise(w1_codes[0], w1_planes[0], w1_bf[0], 0, H)
+        round_w1(1)
+        hyp_bf = keep.tile([P, SLOTS * S], BF16, name="hyp_bf", tag="w2_raw", align_bytes=64)
+        hyp_gain(0, 256)
+        quantise(w1_codes[1], w1_planes[1], w1_bf[1], 0, H)
+        hyp_wide(BANK)
         hyp_gain(256, 512)
-        w1_bf.append(keep.tile([P, SLOTS * H], BF16, name="w1_bf1", tag="hyp_tanh0", align_bytes=64))
-        for t in range(SLOTS):
-            round_w1(1, t, nc.scalar.copy)
+        goal_wide(0, 256)
         quantise(hyp_codes, hyp_planes, hyp_bf, 0, 512)
-        quantise(w1_codes[1], w1_planes[1], w1_bf[1], 0, 256)
-        quantise(w1_codes[1], w1_planes[1], w1_bf[1], 256, 512)
-        for c in range(4, 8):
-            hyp_chunk(c)
-        goal_chunk(0)
-        goal_chunk(1)
         goal_wide(256, 512)
-        hyp_gain(512, 768)
+        weave(goal_bf, goal_rows, 0, 256)
         quantise(goal_codes, goal_planes, goal_bf, 0, 256)
-        hyp_gain(768, 1024)
+        weave(hyp_bf, hyp_rows, 512, 1024)
         goal_wide(512, 1024)
-        goal_weave(256, 512)
+        score(0, 0)
         quantise(hyp_codes, hyp_planes, hyp_bf, 512, 1024)
+        score(1, 0)
+        weave(goal_bf, goal_rows, 256, 512)
+        score(0, 1)
         quantise(goal_codes, goal_planes, goal_bf, 256, 512)
-        score(0)
-        score(1)
-        goal_weave(512, 1024)
-        score(2)
+        score(1, 1)
+        weave(goal_bf, goal_rows, 512, 1024)
+        score(2, 0)
         quantise(goal_codes, goal_planes, goal_bf, 512, 1024)
+        score(2, 1)
         for m in range(3, 8):
-            score(m)
+            score(m, 0)
+            score(m, 1)

from contextlib import ExitStack

import concourse.mybir as mybir
from concourse.masks import make_identity

K, T, S, H = 1024, 2048, 1024, 512
FLOPS = 2 * K * H * S * 2 + 2 * H * S * S

F32 = mybir.dt.float32
BF16 = mybir.dt.bfloat16
I32 = mybir.dt.int32
U32 = mybir.dt.uint32
U16 = mybir.dt.uint16
U8 = mybir.dt.uint8
E4M3 = mybir.dt.float8_e4m3fn_x4
E2M1 = mybir.dt.float4_e2m1fn_x4
ACT = mybir.ActivationFunctionType
ALU = mybir.AluOpType

P = 128
PASSES = 2
SLOTS = 4
CHUNK = 128
BANK = 512


def tile_list_proof_state_pairing_kernel(
    tc, tab_words, tab_scales, offs, w1, w2_words, w2_scales, bias, gain, mask, out
):
    nc = tc.nc
    with ExitStack() as ctx:
        keep = ctx.enter_context(tc.tile_pool(name="keep", bufs=1))
        ring = ctx.enter_context(tc.tile_pool(name="ring", bufs=3))
        psum = ctx.enter_context(tc.psum_pool(name="psum", bufs=8))

        scale_table = keep.tile([P, T], U8, name="scale_table", tag="scale_table", align_bytes=64)
        nc.gpsimd.memset(scale_table[:].bitcast(I32), 0)

        w2_raw = keep.tile([P, PASSES, 256], I32, name="w2_raw", tag="w2_raw", align_bytes=64)
        nc.sync.dma_start(w2_raw[:], w2_words.rearrange("a p c -> p a c").bitcast(I32))
        lists = keep.tile([P, S // 16], U16, name="lists")
        nc.sync.dma_start(lists[:], offs)
        w2s_raw = keep.tile([P, PASSES * H], U8, name="w2s_raw", tag="w2s_raw", align_bytes=64)
        nc.vector.memset(w2s_raw[:].bitcast(I32), 0)
        w2s_rows = w2_scales.rearrange("a (d r) c -> d r a c", r=4)

        def load_w2_scales(d):
            nc.sync.dma_start(
                w2s_raw[32 * d : 32 * d + 4, :].bitcast(I32).rearrange("r (a w) -> r a w", a=PASSES),
                w2s_rows[d].bitcast(I32),
            )

        tab_rows = tab_scales.rearrange("a (g e) t -> a e g t", e=2)
        for a in range(PASSES):
            for e in range(2):
                nc.sync.dma_start(
                    scale_table[2 * a + e : P : 16, :].bitcast(I32), tab_rows[a, e].bitcast(I32)
                )
        table = []
        for a in range(PASSES):
            for d in ((0,), (1, 2, 3))[a]:
                load_w2_scales(d)
            words = keep.tile([P, T], U32, name="table%d" % a, tag="table%d" % a, align_bytes=64)
            nc.sync.dma_start(
                words[:].bitcast(I32), tab_words[a].rearrange("p t i -> p (t i)").bitcast(I32)
            )
            table.append(words)

        coef_rows = keep.tile([P, P], F32, name="coef_rows")
        first = P - 2 * SLOTS
        for i, vec in enumerate((bias, gain)):
            nc.gpsimd.dma_start(
                coef_rows[first + SLOTS * i : first + SLOTS * (i + 1), :].rearrange("t (u l) -> t u l", l=4),
                vec.rearrange("(u t l) -> t u l", t=SLOTS, l=4),
            )

        warm = keep.tile([P, 2], F32, name="warm")
        nc.vector.memset(warm[:, 0:1], 0.0)
        nc.scalar.activation(warm[:, 1:2], warm[:, 0:1], ACT.Sigmoid)

        nc.vector.memset(coef_rows[0:first, :], 0.0)
        v_scales = keep.tile([P, PASSES * S], U8, name="v_scales", align_bytes=64)
        nc.vector.memset(v_scales[:, S : 2 * S].bitcast(I32), 0)
        w2_planes = keep.tile([P, PASSES * H], U8, name="w2_planes", align_bytes=64)

        ident = keep.tile([P, P], F32, name="ident")
        make_identity(nc, ident[:])

        picked_scales = keep.tile([P, S], U8, name="picked_scales", align_bytes=64)
        nc.vector.tensor_copy(picked_scales[:], scale_table[:].indirect(lists[:]))
        nc.vector.tensor_copy(v_scales[:, 0:S].bitcast(I32), picked_scales[:].bitcast(I32))
        for a in range(PASSES):
            for r in range(4):
                if a > 0 or r >= 2:
                    nc.sync.dma_start(
                        v_scales[r:P:32, a * S : (a + 1) * S].bitcast(I32),
                        picked_scales[16 * (r // 2) + 2 * a + r % 2 : P : 32, :].bitcast(I32),
                    )
        w1_raw = []
        raw0 = keep.tile([P, SLOTS * H], F32, name="w1_raw0", tag="scale_table", align_bytes=64)
        nc.sync.dma_start(raw0[:], w1[0:512, :].rearrange("(p j) c -> p (j c)", j=4))
        w1_raw.append(raw0)

        coef_bank = psum.tile([P, BANK], F32, name="coef_bank", tag="bank")
        nc.tensor.transpose(coef_bank[:, 0:P], coef_rows[:], ident[:])
        coef = keep.tile([P, 2 * SLOTS], F32, name="coef")
        nc.scalar.copy(coef[:], coef_bank[:, first:P])

        v_words = [keep.tile([P, S], U32, name="v_words0", align_bytes=64)]
        nc.vector.tensor_copy(v_words[0][:], table[0][:].indirect(lists[:]))

        nc.vector.tensor_copy(
            w2_planes[:].bitcast(I32).rearrange("p (a t u) -> p a t u", a=PASSES, t=SLOTS),
            w2s_raw[:].bitcast(I32).rearrange("p (a u t) -> p a t u", a=PASSES, t=SLOTS),
        )
        w2_codes = keep.tile([P, PASSES * 2 * H], U8, name="w2_codes", tag="table0", align_bytes=64)
        nc.vector.tensor_copy(
            w2_codes[:].bitcast(I32).rearrange("p (a t u w) -> p a t u w", a=PASSES, t=SLOTS, w=2),
            w2_raw[:].rearrange("p a (u t w) -> p a t u w", t=SLOTS, w=2),
        )
        raw1 = keep.tile([P, SLOTS * H], F32, name="w1_raw1", tag="w2_raw", align_bytes=64)
        nc.sync.dma_start(raw1[:], w1[512:1024, :].rearrange("(p j) c -> p (j c)", j=4))
        w1_raw.append(raw1)

        v_words.append(keep.tile([P, S], U32, name="v_words1", align_bytes=64))
        for c0, c1 in ((0, 256), (256, 512), (512, 1024)):
            nc.vector.tensor_copy(
                v_words[1][:, c0:c1], table[1][:].indirect(lists[:, c0 // 16 : c1 // 16])
            )

        masks_sb = keep.tile([P, S // P, S], F32, name="masks_sb", tag="table1", align_bytes=64)
        for m in range(S // P):
            nc.sync.dma_start(masks_sb[:, m, :], mask[m * P : (m + 1) * P, :])

        w1_bf = [keep.tile([P, SLOTS * H], BF16, name="w1_bf%d" % a, align_bytes=64) for a in range(PASSES)]
        w1_codes = [keep.tile([P, H], U32, name="w1_codes%d" % a, align_bytes=64) for a in range(PASSES)]
        w1_planes = [keep.tile([P, H], U8, name="w1_planes%d" % a, align_bytes=64) for a in range(PASSES)]

        def round_w1(a):
            nc.vector.tensor_copy(
                w1_bf[a][:].rearrange("p (t u l j) -> p t u j l", t=SLOTS, l=4, j=4),
                w1_raw[a][:].rearrange("p (j u t l) -> p t u j l", t=SLOTS, l=4, j=4),
            )

        def quantise(codes, planes, values, c0, c1):
            nc.vector.quantize_mx(
                out=codes[:, c0:c1].bitcast(E4M3), scales=planes[:, c0:c1], in_=values[:, 4 * c0 : 4 * c1]
            )

        def w1_operand(a, t):
            cols = slice(t * P, (t + 1) * P)
            return w1_codes[a][:, cols].bitcast(E4M3), w1_planes[a][:, cols]

        def w2_operand(a, t):
            col = a * H + t * P
            return w2_codes[:, 2 * col : 2 * (col + P)].bitcast(E2M1), w2_planes[:, col : col + P]

        def project(bank_cols, operand, t, c0, c1):
            for a in range(PASSES):
                codes, plane = operand(a, t)
                nc.tensor.matmul_mx(
                    out=bank_cols,
                    lhsT=codes,
                    lhsT_scale=plane,
                    rhs=v_words[a][:, c0:c1].bitcast(E4M3),
                    rhs_scale=v_scales[:, a * S + c0 : a * S + c1],
                    start=(a == 0),
                    stop=(a == PASSES - 1),
                )

        def project_narrow(operand, c0):
            bank = psum.tile([P, BANK], F32, name="bank", tag="bank")
            for t in range(SLOTS):
                project(bank[:, t * CHUNK : (t + 1) * CHUNK], operand, t, c0, c0 + CHUNK)
            return bank[:].rearrange("p (t n) -> p n t", t=SLOTS)

        def woven(tile, c0, c1):
            return tile[:, 4 * c0 : 4 * c1].rearrange("p (n t) -> p n t", t=SLOTS)

        def weave(dst, rows, c0, c1):
            nc.vector.tensor_copy(
                dst[:, 4 * c0 : 4 * c1].rearrange("p (n l t) -> p n t l", t=SLOTS, l=4),
                rows[:, 4 * c0 : 4 * c1].rearrange("p (t n l) -> p n t l", t=SLOTS, l=4),
            )

        hyp_tanh = keep.tile([P, SLOTS * S], F32, name="hyp_tanh")
        hyp_rows = keep.tile([P, SLOTS * S], BF16, name="hyp_rows")
        hyp_codes = keep.tile([P, S], U32, name="hyp_codes", align_bytes=64)
        hyp_planes = keep.tile([P, S], U8, name="hyp_planes", align_bytes=64)
        goal_rows = keep.tile([P, SLOTS * S], BF16, name="goal_rows")
        goal_bf = keep.tile([P, SLOTS * S], BF16, name="goal_bf", align_bytes=64)
        goal_codes = keep.tile([P, S], U32, name="goal_codes", align_bytes=64)
        goal_planes = keep.tile([P, S], U8, name="goal_planes", align_bytes=64)

        def hyp_narrow(c0):
            nc.scalar.activation(woven(hyp_tanh, c0, c0 + CHUNK), project_narrow(w2_operand, c0), ACT.Tanh)

        def hyp_gain(c0, c1):
            nc.vector.tensor_tensor(
                woven(hyp_bf, c0, c1),
                woven(hyp_tanh, c0, c1),
                coef[:, SLOTS : 2 * SLOTS].unsqueeze(1).to_broadcast([P, c1 - c0, SLOTS]),
                ALU.mult,
            )

        def hyp_wide(c0):
            for t in range(SLOTS):
                bank = psum.tile([P, BANK], F32, name="bank", tag="bank")
                project(bank[:], w2_operand, t, c0, c0 + BANK)
                row = slice(4 * c0 + t * BANK, 4 * c0 + (t + 1) * BANK)
                nc.scalar.activation(hyp_tanh[:, row], bank[:], ACT.Tanh)
                nc.scalar.activation(
                    hyp_rows[:, row], hyp_tanh[:, row], ACT.Copy, scale=coef[:, SLOTS + t : SLOTS + t + 1]
                )

        def goal_narrow(c0):
            nc.vector.tensor_tensor(
                woven(goal_bf, c0, c0 + CHUNK),
                project_narrow(w1_operand, c0),
                coef[:, 0:SLOTS].unsqueeze(1).to_broadcast([P, CHUNK, SLOTS]),
                ALU.add,
            )

        def goal_wide(c0, c1):
            width = c1 - c0
            per_bank = BANK // width
            for t0 in range(0, SLOTS, per_bank):
                bank = psum.tile([P, BANK], F32, name="bank", tag="bank")
                for t in range(t0, t0 + per_bank):
                    project(bank[:, (t - t0) * width : (t - t0 + 1) * width], w1_operand, t, c0, c1)
                for t in range(t0, t0 + per_bank):
                    nc.scalar.activation(
                        goal_rows[:, 4 * c0 + t * width : 4 * c0 + (t + 1) * width],
                        bank[:, (t - t0) * width : (t - t0 + 1) * width],
                        ACT.Identity,
                        bias=coef[:, t : t + 1],
                    )

        results = {}

        def score(m, h):
            if m not in results:
                results[m] = ring.tile([P, S], F32, name="result", bufs=4)
            result = results[m]
            rows, cols = slice(m * P, (m + 1) * P), slice(h * BANK, (h + 1) * BANK)
            bank = psum.tile([P, BANK], F32, name="bank", tag="bank")
            nc.tensor.matmul_mx(
                out=bank[:],
                lhsT=goal_codes[:, rows].bitcast(E4M3),
                lhsT_scale=goal_planes[:, rows],
                rhs=hyp_codes[:, cols].bitcast(E4M3),
                rhs_scale=hyp_planes[:, cols],
                start=True,
                stop=True,
            )
            last = m == S // P - 1 and h == 1
            width = BANK // 2 if last else BANK
            for u0 in range(0, BANK, width):
                part = slice(h * BANK + u0, h * BANK + u0 + width)
                logits = ring.tile([P, width], F32, name="logits", bufs=6)
                nc.vector.tensor_tensor(logits[:], bank[:, u0 : u0 + width], masks_sb[:, m, part], ALU.add)
                nc.scalar.activation(result[:, part], logits[:], ACT.Sigmoid)
                if m >= S // P - 2:
                    nc.sync.dma_start(out[rows, part], result[:, part])
            if m < S // P - 2 and h == 1:
                nc.sync.dma_start(out[rows, :], result[:])

        round_w1(0)
        for c0 in range(0, BANK, CHUNK):
            hyp_narrow(c0)
        quantise(w1_codes[0], w1_planes[0], w1_bf[0], 0, H)
        round_w1(1)
        hyp_bf = keep.tile([P, SLOTS * S], BF16, name="hyp_bf", tag="w2_raw", align_bytes=64)
        hyp_gain(0, 256)
        quantise(w1_codes[1], w1_planes[1], w1_bf[1], 0, H)
        hyp_wide(BANK)
        hyp_gain(256, 512)
        goal_wide(0, 256)
        quantise(hyp_codes, hyp_planes, hyp_bf, 0, 512)
        goal_wide(256, 512)
        weave(goal_bf, goal_rows, 0, 256)
        quantise(goal_codes, goal_planes, goal_bf, 0, 256)
        weave(hyp_bf, hyp_rows, 512, 1024)
        goal_wide(512, 1024)
        score(0, 0)
        quantise(hyp_codes, hyp_planes, hyp_bf, 512, 1024)
        score(1, 0)
        weave(goal_bf, goal_rows, 256, 512)
        score(0, 1)
        quantise(goal_codes, goal_planes, goal_bf, 256, 512)
        score(1, 1)
        weave(goal_bf, goal_rows, 512, 1024)
        score(2, 0)
        quantise(goal_codes, goal_planes, goal_bf, 512, 1024)
        score(2, 1)
        for m in range(3, 8):
            score(m, 0)
            score(m, 1)
